import numpy as np
import ml_dtypes


def mxq(x, axis, fmt="e4m3"):
    dtype, down = {"e4m3": (ml_dtypes.float8_e4m3fn, 7), "e5m2": (ml_dtypes.float8_e5m2, 14)}[fmt]
    v = np.moveaxis(np.asarray(x, np.float32).astype(ml_dtypes.bfloat16).astype(np.float64), axis, -1)
    blocks = v.reshape(v.shape[:-1] + (-1, 32))
    amax = np.abs(blocks).max(-1, keepdims=True)
    byte = np.maximum(np.where(amax > 0, np.frexp(amax)[1] - 1 + 127, 0) - down, 1)
    scale = np.exp2(byte - 127.0)
    codes = (blocks / scale).astype(np.float32).astype(dtype).astype(np.float64)
    return np.moveaxis((codes * scale).reshape(v.shape), -1, axis)


WIDE = False


def mx_kscale(k):
    if not WIDE:
        return np.ones(k)
    levels = np.array([10, -10, 5, -5, 0])
    if k % 512:
        return np.exp2(np.random.permutation(np.resize(levels, k // 32))).repeat(32)
    a = np.empty((k // 512, 16))
    for p in range(k // 512):
        a[p, :8] = np.random.permutation(np.resize(levels, 8))
        for g in range(8):
            far = levels[np.abs(levels - a[p, g]) >= 10]
            a[p, g + 8] = far[np.random.randint(len(far))]
    return np.exp2(a.ravel()).repeat(32)


def f64(x):
    return np.asarray(x).astype(np.float64)


def striped(idx):
    return np.tile(idx.reshape(-1, 16).T, (8, 1)).astype(np.uint16)


def unstriped(offs):
    return offs[:16].T.reshape(-1).astype(np.int64)


def pack_weight(w):
    k, n = w.shape
    w = f64(np.asarray(w, np.float32).astype(ml_dtypes.bfloat16)).reshape(k // 32, 32, n)
    amax = np.abs(w).max(1)
    byte = np.clip(np.where(amax > 0, np.frexp(amax)[1] - 1 + 127 - 7, 1), 1, 254)
    scaled = (w * np.exp2(127.0 - byte)[:, None, :]).reshape(k, n).astype(np.float32)
    words = np.ascontiguousarray(scaled.reshape(k // 512, 128, 4, n).transpose(0, 1, 3, 2)).astype(ml_dtypes.float8_e4m3fn).view(np.uint8)
    return words, np.ascontiguousarray(byte.astype(np.uint8).reshape(k // 512, 16, n))


def unpack_weight(words, scales):
    g, p, n, _ = words.shape
    vals = np.ascontiguousarray(words).view(ml_dtypes.float8_e4m3fn).astype(np.float64) * np.repeat(np.exp2(scales.astype(np.float64) - 127.0), 8, axis=1)[..., None]
    return vals.transpose(0, 1, 3, 2).reshape(g * 512, n)


E2M1 = np.array([0.0, 0.5, 1.0, 1.5, 2.0, 3.0, 4.0, 6.0, -0.0, -0.5, -1.0, -1.5, -2.0, -3.0, -4.0, -6.0])


def pack_fp4(w):
    k, n = w.shape
    w = f64(np.asarray(w, np.float32).astype(ml_dtypes.bfloat16)).reshape(k // 32, 32, n)
    amax = np.abs(w).max(1)
    mant, ex = np.frexp(amax / 6.0)
    byte = np.clip(np.where(amax > 0, np.where(mant > 0.5, ex, ex - 1) + 127, 1), 1, 254)
    scaled = (w * np.exp2(127.0 - byte)[:, None, :]).reshape(k, n).astype(np.float32)
    c = np.ascontiguousarray(scaled.reshape(k // 512, 128, 4, n).transpose(0, 1, 3, 2)).astype(ml_dtypes.float4_e2m1fn).view(np.uint8) & 0xF
    words = (c[..., 0::2] | (c[..., 1::2] << 4)).reshape(k // 512, 128, 2 * n)
    return np.ascontiguousarray(words), np.ascontiguousarray(byte.astype(np.uint8).reshape(k // 512, 16, n))


def unpack_fp4(words, scales):
    g, _, n = scales.shape
    words = np.ascontiguousarray(words).reshape(g, 128, n, 2)
    nib = np.empty((g, 128, n, 4), np.uint8)
    nib[..., 0::2] = words & 0xF
    nib[..., 1::2] = words >> 4
    vals = E2M1[nib] * np.repeat(np.exp2(scales.astype(np.float64) - 127.0), 8, axis=1)[..., None]
    return vals.transpose(0, 1, 3, 2).reshape(g * 512, n)


def planes(y):
    n, m = y.shape
    v = y.astype(np.float32).astype(ml_dtypes.bfloat16).astype(np.float64).reshape(n // 32, 32, m)
    top = np.abs(v).max(1)
    byte = np.clip(np.where(top > 0, np.frexp(top)[1] - 1 + 127 - 7, 1), 1, 254)
    codes = (v * np.exp2(127.0 - byte)[:, None, :]).reshape(n, m).astype(np.float32).astype(ml_dtypes.float8_e4m3fn).view(np.uint8)
    words = codes.reshape(n // 512, 128, 4, m).transpose(0, 1, 3, 2)
    return np.ascontiguousarray(words), np.ascontiguousarray(byte.astype(np.uint8).reshape(n // 512, 16, m))


K, T, S, H, N, V = 1024, 2048, 1024, 512, 512, 512
P = 2 ** 7


def setup_inputs():
    n = np.random.standard_normal
    s = mx_kscale(K)[:, None]
    u = mx_kscale(H)
    perm = np.random.permutation(S)
    packed_xT = pack_weight(n((K, T)) * s)
    packed_w2 = pack_fp4(n((H, N)) / np.sqrt(H) / u[:, None])
    return {
        "x_words": packed_xT[0],
        "x_scales": packed_xT[1],
        "w1": (n((K, H)) / np.sqrt(K) / s * u).astype(np.float32),
        "w2_words": packed_w2[0],
        "w2_scales": packed_w2[1],
        "gate": (np.tile(np.random.uniform(0.2, 1.0, V), (P, 1))).astype(np.float32),
        "back": (np.tile(np.random.uniform(0.5, 1.5, V), (P, 1))).astype(np.float32),
        "offs": striped(np.random.permutation(T)[:S]),
        "ka": striped(perm[:V]),
        "kb": striped(perm[V:]),
    }


def reference(x_words, x_scales, w1, w2_words, w2_scales, gate, back, offs, ka, kb):
    xq = unpack_weight(x_words, x_scales)[:, unstriped(offs)]
    h = mxq(f64(w1), 0, "e4m3").T @ xq
    z = h[:, unstriped(ka)] + h[:, unstriped(kb)] * f64(gate)[:1]
    y = unpack_fp4(w2_words, w2_scales).T @ mxq(z, 0, "e4m3")
    yb = y * f64(back)[:1]
    out = np.zeros((H, S))
    out[:, unstriped(ka)] = y
    res = out.copy()
    res[:, unstriped(kb)] = yb
    out_0 = res
    return (out_0,) + planes(out_0)

@@ -1,0 +1,252 @@
+from contextlib import ExitStack
+
+import concourse.mybir as mybir
+
+K, T, S, H, N, V = 1024, 2048, 1024, 512, 512, 512
+FLOPS = 2 * K * H * S + 2 * H * N * V
+
+F32 = mybir.dt.float32
+BF16 = mybir.dt.bfloat16
+I32 = mybir.dt.int32
+U32 = mybir.dt.uint32
+U16 = mybir.dt.uint16
+U8 = mybir.dt.uint8
+FP8X4 = mybir.dt.float8_e4m3fn_x4
+FP4X4 = mybir.dt.float4_e2m1fn_x4
+MULT = mybir.AluOpType.mult
+ADD = mybir.AluOpType.add
+COPY = mybir.ActivationFunctionType.Copy
+
+P = 128
+PACK = 4
+PASSES = K // (P * PACK)
+BANK = 512
+HALF = V // 2
+STRIPE = 16
+SPLIT = 640
+
+
+def tile_picked_zunm_none_po_kernel(
+    tc, x_words, x_scales, w1, w2_words, w2_scales, gate, back, offs, ka, kb, out_0, out_1, out_2
+):
+    nc = tc.nc
+    with ExitStack() as ctx:
+        sb = ctx.enter_context(tc.tile_pool(name="sb", bufs=1))
+        psum = ctx.enter_context(tc.psum_pool(name="psum", bufs=1))
+
+        def new(shape, dtype, name):
+            return sb.tile(shape, dtype, name=name, align_bytes=64)
+
+        offs_t = sb.tile([P, S // STRIPE], U16, name="offs_t")
+        ka_t = sb.tile([P, V // STRIPE], U16, name="ka_t")
+        kb_t = sb.tile([P, V // STRIPE], U16, name="kb_t")
+
+        xw = [new([P, T], U32, "xw%d" % g) for g in range(PASSES)]
+        xs = new([P, T], U8, "xs")
+        w1_raw = [[new([P, PACK, H // 2], F32, "w1_raw%d%d" % (g, e)) for e in range(2)] for g in range(PASSES)]
+        w2w_raw = new([P, 2 * N], U8, "w2w_raw")
+        w2s_raw = new([P, N], U8, "w2s_raw")
+        gate_t = new([P, V], F32, "gate_t")
+        back_t = new([P, V], F32, "back_t")
+
+        def load_x(g):
+            nc.sync.dma_start(out=xw[g][:].bitcast(I32), in_=x_words[g].rearrange("p n t -> p (n t)").bitcast(I32))
+
+        def load_w1(g):
+            for e in range(2):
+                rows = w1[g * 512 : (g + 1) * 512, e * (H // 2) : (e + 1) * (H // 2)]
+                nc.sync.dma_start(out=w1_raw[g][e][:], in_=rows.rearrange("(p j) c -> p j c", j=PACK))
+
+        nc.gpsimd.memset(xs[:].bitcast(I32), 0)
+        nc.gpsimd.memset(w2s_raw[:].bitcast(I32), 0)
+        nc.sync.dma_start(out=offs_t[:], in_=offs)
+        load_x(0)
+        for q in range(4):
+            nc.sync.dma_start(
+                out=xs[32 * q : 32 * q + 4 * PASSES, :].bitcast(I32), in_=x_scales[:, 4 * q : 4 * q + 4, :].bitcast(I32)
+            )
+        load_w1(0)
+        load_x(1)
+        load_w1(1)
+        nc.sync.dma_start(out=w2w_raw[:].bitcast(I32), in_=w2_words[0].bitcast(I32))
+        nc.sync.dma_start(out=kb_t[:], in_=kb)
+        nc.sync.dma_start(out=ka_t[:], in_=ka)
+        nc.sync.dma_start(out=gate_t[:], in_=gate)
+        for q in range(4):
+            nc.sync.dma_start(
+                out=w2s_raw[32 * q : 32 * q + 4, :].bitcast(I32), in_=w2_scales[0, 4 * q : 4 * q + 4, :].bitcast(I32)
+            )
+        nc.sync.dma_start(out=back_t[:], in_=back)
+
+        w1_bf = [[new([P, 2 * P * PACK], BF16, "w1_bf%d%d" % (g, u)) for u in range(2)] for g in range(PASSES)]
+        w1_codes = [[new([P, 2 * P], U32, "w1_codes%d%d" % (g, u)) for u in range(2)] for g in range(PASSES)]
+        w1_scales = [[new([P, 2 * P], U8, "w1_scales%d%d" % (g, u)) for u in range(2)] for g in range(PASSES)]
+
+        def round_w1(copy, g, e, u):
+            copy(
+                out=w1_bf[g][u][:].rearrange("p (t m j) -> p m j t", t=2, j=PACK)[:, e * (P // 2) : (e + 1) * (P // 2), :, :],
+                in_=w1_raw[g][e][:].rearrange("p j (m t) -> p m j t", t=PACK)[:, :, :, 2 * u : 2 * u + 2],
+            )
+
+        def quantise_w1(g, u):
+            nc.vector.quantize_mx(out=w1_codes[g][u][:].bitcast(FP8X4), scales=w1_scales[g][u][:], in_=w1_bf[g][u][:])
+
+        gs = new([P, S], U8, "gs")
+        gw = [new([P, S], U32, "gw%d" % g) for g in range(PASSES)]
+        h_ps = [[psum.tile([P, BANK], F32, name="h_ps%d%d" % (t, c), tag="bank%d" % (2 * t + c)) for c in range(2)] for t in range(PACK)]
+
+        def product1(g, t, c):
+            cols = slice((t % 2) * P, (t % 2 + 1) * P)
+            picked = slice(c * BANK, (c + 1) * BANK)
+            nc.tensor.matmul_mx(
+                out=h_ps[t][c][:],
+                lhsT=w1_codes[g][t // 2][:, cols].bitcast(FP8X4),
+                lhsT_scale=w1_scales[g][t // 2][:, cols],
+                rhs=gw[g][:, picked].bitcast(FP8X4),
+                rhs_scale=gs[4 * g : P, picked],
+                start=(g == 0),
+                stop=(g == PASSES - 1),
+            )
+
+        for e in range(2):
+            for u in range(2):
+                round_w1(nc.scalar.copy, 0, e, u)
+        nc.vector.tensor_copy(out=gw[0][:], in_=xw[0][:].indirect(offs_t[:]))
+        nc.vector.tensor_copy(out=gs[:], in_=xs[:].indirect(offs_t[:]))
+        quantise_w1(0, 0)
+        quantise_w1(0, 1)
+        for t in range(PACK):
+            for c in range(2):
+                product1(0, t, c)
+        nc.vector.tensor_copy(out=gw[1][:], in_=xw[1][:].indirect(offs_t[:]))
+        round_w1(nc.scalar.copy, 1, 0, 0)
+        round_w1(nc.scalar.copy, 1, 0, 1)
+        round_w1(nc.vector.tensor_copy, 1, 1, 0)
+        round_w1(nc.scalar.copy, 1, 1, 1)
+        quantise_w1(1, 0)
+        quantise_w1(1, 1)
+        for t in range(PACK):
+            for c in range(2):
+                product1(1, t, c)
+
+        h = [new([P, S], F32, "h%d" % t) for t in range(PACK)]
+        for t in range(PACK):
+            for c in range(2):
+                copy = nc.vector.tensor_copy if (c == 1 and t < 3) else nc.scalar.copy
+                copy(out=h[t][:, c * BANK : (c + 1) * BANK], in_=h_ps[t][c][:])
+
+        w2w = new([P, 2 * N], U8, "w2w")
+        w2s = new([P, N], U8, "w2s")
+        nc.scalar.copy(
+            out=w2w[:].bitcast(U16).rearrange("p (t m) -> p m t", t=PACK),
+            in_=w2w_raw[:].bitcast(U16).rearrange("p (m t) -> p m t", t=PACK),
+        )
+
+        nc.vector.tensor_copy(
+            out=w2s[:].rearrange("p (t m) -> p t m", t=PACK), in_=w2s_raw[:].rearrange("p (m t) -> p t m", t=PACK)
+        )
+        per = HALF // STRIPE
+        y = [[new([P, 2 * HALF], F32, "y%d%d" % (a, u)) for u in range(2)] for a in range(2)]
+        y_ps = [[None, None], [None, None]]
+
+        def merge(a):
+            first = new([P, PACK, HALF], F32, "first%d" % a)
+            second = new([P, PACK, HALF], F32, "second")
+            z_bf = new([P, HALF * PACK], BF16, "z_bf%d" % a)
+            z_codes = new([P, HALF], U32, "z_codes%d" % a)
+            z_scales = new([P, HALF], U8, "z_scales%d" % a)
+            for t in range(PACK):
+                nc.scalar.activation(out=first[:, t, :], in_=h[t][:].indirect(ka_t[:, a * per : (a + 1) * per]), func=COPY)
+                nc.vector.tensor_tensor(
+                    out=second[:, t, :],
+                    in0=h[t][:].indirect(kb_t[:, a * per : (a + 1) * per]),
+                    in1=gate_t[:, a * HALF : (a + 1) * HALF],
+                    op=MULT,
+                )
+            nc.vector.tensor_tensor(
+                out=z_bf[:].rearrange("p (c i t) -> p c t i", i=4, t=PACK),
+                in0=first[:].rearrange("p t (c i) -> p c t i", i=4),
+                in1=second[:].rearrange("p t (c i) -> p c t i", i=4),
+                op=ADD,
+            )
+            nc.vector.quantize_mx(out=z_codes[:].bitcast(FP8X4), scales=z_scales[:], in_=z_bf[:])
+            for u in range(2):
+                y_ps[a][u] = psum.tile([P, BANK], F32, name="y_ps%d%d" % (a, u), tag="bank%d" % (2 * a + u))
+                for e in range(2):
+                    t = 2 * u + e
+                    nc.tensor.matmul_mx(
+                        out=y_ps[a][u][:, e * HALF : (e + 1) * HALF],
+                        lhsT=w2w[:, 2 * P * t : 2 * P * (t + 1)].bitcast(FP4X4),
+                        lhsT_scale=w2s[:, P * t : P * (t + 1)],
+                        rhs=z_codes[:].bitcast(FP8X4),
+                        rhs_scale=z_scales[:],
+                        start=True,
+                        stop=True,
+                    )
+
+        def take_y(a, u):
+            nc.scalar.copy(out=y[a][u][:], in_=y_ps[a][u][:])
+
+        res = [new([P, S], F32, "res%d" % t) for t in range(PACK)]
+        widths = (SPLIT, S - SPLIT)
+        starts = (0, SPLIT)
+        grouped = [new([P, PACK, widths[r]], F32, "grouped%d" % r) for r in range(2)]
+        out_rows = out_0.rearrange("(p t) s -> p t s", t=PACK)
+
+        def put_first(a, t):
+            src = y[a][t // 2][:, (t % 2) * HALF : (t % 2 + 1) * HALF]
+            nc.scalar.activation(out=res[t][:].indirect(ka_t[:, a * per : (a + 1) * per]), in_=src, func=COPY)
+
+        def put_second(a, t):
+            nc.vector.tensor_tensor(
+                out=res[t][:].indirect(kb_t[:, a * per : (a + 1) * per]),
+                in0=y[a][t // 2][:, (t % 2) * HALF : (t % 2 + 1) * HALF],
+                in1=back_t[:, a * HALF : (a + 1) * HALF],
+                op=MULT,
+            )
+
+        def regroup(move, t, r):
+            move(out=grouped[r][:, t, :], in_=res[t][:, starts[r] : starts[r] + widths[r]])
+
+        def store(t):
+            nc.sync.dma_start(out=out_rows[:, t, :], in_=res[t][:])
+
+        merge(0)
+        merge(1)
+        for u in range(2):
+            take_y(0, u)
+            for t in (2 * u, 2 * u + 1):
+                put_first(0, t)
+                put_second(0, t)
+        for u in range(2):
+            take_y(1, u)
+            put_first(1, 2 * u)
+            put_second(1, 2 * u + 1)
+            put_first(1, 2 * u + 1)
+            put_second(1, 2 * u)
+            for t in (2 * u, 2 * u + 1):
+                regroup(nc.sync.dma_start if u == 0 else nc.vector.tensor_copy, t, 0)
+                regroup(nc.sync.dma_start if u == 0 else nc.scalar.copy, t, 1)
+            for t in (2 * u, 2 * u + 1):
+                store(t)
+
+        o_codes = new([P, S], U32, "o_codes")
+        o_scales = new([P, S], U8, "o_scales")
+        pieces = ((0, 0, 256), (0, 256, SPLIT - 256), (1, 0, S - SPLIT))
+        o_bf = [new([P, PACK * w], BF16, "o_bf%d" % i) for i, (r, c0, w) in enumerate(pieces)]
+        for i, (r, c0, w) in enumerate(pieces):
+            copy = nc.vector.tensor_copy if r == 0 else nc.scalar.copy
+            copy(
+                out=o_bf[i][:].rearrange("p (c i t) -> p c t i", i=4, t=PACK),
+                in_=grouped[r][:, :, c0 : c0 + w].rearrange("p t (c i) -> p c t i", i=4),
+            )
+        words_out = out_1[0].rearrange("p n t -> p (n t)").bitcast(I32)
+        for i, (r, c0, w) in enumerate(pieces):
+            cols = slice(starts[r] + c0, starts[r] + c0 + w)
+            nc.vector.quantize_mx(out=o_codes[:, cols].bitcast(FP8X4), scales=o_scales[:, cols], in_=o_bf[i][:])
+            nc.sync.dma_start(out=words_out[:, cols], in_=o_codes[:, cols].bitcast(I32))
+        for q in range(4):
+            queue = nc.scalar if q % 2 else nc.sync
+            queue.dma_start(
+                out=out_2[0, 4 * q : 4 * q + 4, :].bitcast(I32), in_=o_scales[32 * q : 32 * q + 4, :].bitcast(I32)
+            )

@@ -34,15 +34,15 @@ def tile_picked_zunm_none_po_kernel(
         sb = ctx.enter_context(tc.tile_pool(name="sb", bufs=1))
         psum = ctx.enter_context(tc.psum_pool(name="psum", bufs=1))
 
-        def new(shape, dtype, name):
-            return sb.tile(shape, dtype, name=name, align_bytes=64)
+        def new(shape, dtype, name, tag=""):
+            return sb.tile(shape, dtype, name=name, tag=tag, align_bytes=64)
 
         offs_t = sb.tile([P, S // STRIPE], U16, name="offs_t")
         ka_t = sb.tile([P, V // STRIPE], U16, name="ka_t")
         kb_t = sb.tile([P, V // STRIPE], U16, name="kb_t")
 
         xw = [new([P, T], U32, "xw%d" % g) for g in range(PASSES)]
-        xs = new([P, T], U8, "xs")
+        xs = new([P, T], U8, "xs", "gw1")
         w1_raw = [[new([P, PACK, H // 2], F32, "w1_raw%d%d" % (g, e)) for e in range(2)] for g in range(PASSES)]
         w2w_raw = new([P, 2 * N], U8, "w2w_raw")
         w2s_raw = new([P, N], U8, "w2s_raw")
@@ -57,10 +57,11 @@ def tile_picked_zunm_none_po_kernel(
                 rows = w1[g * 512 : (g + 1) * 512, e * (H // 2) : (e + 1) * (H // 2)]
                 nc.sync.dma_start(out=w1_raw[g][e][:], in_=rows.rearrange("(p j) c -> p j c", j=PACK))
 
-        nc.gpsimd.memset(xs[:].bitcast(I32), 0)
+        nc.vector.memset(xs[:, :1408].bitcast(I32), 0)
+        nc.gpsimd.memset(xs[:, 1408:].bitcast(I32), 0)
         nc.gpsimd.memset(w2s_raw[:].bitcast(I32), 0)
-        nc.sync.dma_start(out=offs_t[:], in_=offs)
         load_x(0)
+        nc.sync.dma_start(out=offs_t[:], in_=offs)
         for q in range(4):
             nc.sync.dma_start(
                 out=xs[32 * q : 32 * q + 4 * PASSES, :].bitcast(I32), in_=x_scales[:, 4 * q : 4 * q + 4, :].bitcast(I32)
@@ -78,12 +79,12 @@ def tile_picked_zunm_none_po_kernel(
             )
         nc.sync.dma_start(out=back_t[:], in_=back)
 
-        w1_bf = [[new([P, 2 * P * PACK], BF16, "w1_bf%d%d" % (g, u)) for u in range(2)] for g in range(PASSES)]
+        w1_bf = [[new([P, 2 * P * PACK], BF16, "w1_bf%d%d" % (g, u), "w1_bf%d%d" % (g, u)) for u in range(2)] for g in range(PASSES)]
         w1_codes = [[new([P, 2 * P], U32, "w1_codes%d%d" % (g, u)) for u in range(2)] for g in range(PASSES)]
         w1_scales = [[new([P, 2 * P], U8, "w1_scales%d%d" % (g, u)) for u in range(2)] for g in range(PASSES)]
 
-        def round_w1(copy, g, e, u):
-            copy(
+        def round_w1(g, e, u):
+            nc.scalar.copy(
                 out=w1_bf[g][u][:].rearrange("p (t m j) -> p m j t", t=2, j=PACK)[:, e * (P // 2) : (e + 1) * (P // 2), :, :],
                 in_=w1_raw[g][e][:].rearrange("p j (m t) -> p m j t", t=PACK)[:, :, :, 2 * u : 2 * u + 2],
             )
@@ -91,38 +92,43 @@ def tile_picked_zunm_none_po_kernel(
         def quantise_w1(g, u):
             nc.vector.quantize_mx(out=w1_codes[g][u][:].bitcast(FP8X4), scales=w1_scales[g][u][:], in_=w1_bf[g][u][:])
 
-        gs = new([P, S], U8, "gs")
-        gw = [new([P, S], U32, "gw%d" % g) for g in range(PASSES)]
+        gs = [None, None]
+        gw = [[new([P, BANK], U32, "gw0%d" % c)[:] for c in range(2)], None]
+        half_list = [offs_t[:, c * (BANK // STRIPE) : (c + 1) * (BANK // STRIPE)] for c in range(2)]
         h_ps = [[psum.tile([P, BANK], F32, name="h_ps%d%d" % (t, c), tag="bank%d" % (2 * t + c)) for c in range(2)] for t in range(PACK)]
 
         def product1(g, t, c):
             cols = slice((t % 2) * P, (t % 2 + 1) * P)
-            picked = slice(c * BANK, (c + 1) * BANK)
             nc.tensor.matmul_mx(
                 out=h_ps[t][c][:],
                 lhsT=w1_codes[g][t // 2][:, cols].bitcast(FP8X4),
                 lhsT_scale=w1_scales[g][t // 2][:, cols],
-                rhs=gw[g][:, picked].bitcast(FP8X4),
-                rhs_scale=gs[4 * g : P, picked],
+                rhs=gw[g][c].bitcast(FP8X4),
+                rhs_scale=gs[c][4 * g : P, :],
                 start=(g == 0),
                 stop=(g == PASSES - 1),
             )
 
         for e in range(2):
             for u in range(2):
-                round_w1(nc.scalar.copy, 0, e, u)
-        nc.vector.tensor_copy(out=gw[0][:], in_=xw[0][:].indirect(offs_t[:]))
-        nc.vector.tensor_copy(out=gs[:], in_=xs[:].indirect(offs_t[:]))
+                round_w1(0, e, u)
+        gs[0] = new([P, BANK], U8, "gs0", "gs0")
+        nc.vector.tensor_copy(out=gw[0][0], in_=xw[0][:].indirect(half_list[0]))
+        nc.vector.tensor_copy(out=gs[0][:], in_=xs[:].indirect(half_list[0]))
+        nc.vector.tensor_copy(out=gw[0][1], in_=xw[0][:].indirect(half_list[1]))
         quantise_w1(0, 0)
         quantise_w1(0, 1)
-        for t in range(PACK):
-            for c in range(2):
+        gs[1] = new([P, BANK], U8, "gs1", "w1_bf00")
+        nc.vector.tensor_copy(out=gs[1][:], in_=xs[:].indirect(half_list[1]))
+        for c in range(2):
+            for t in range(PACK):
                 product1(0, t, c)
-        nc.vector.tensor_copy(out=gw[1][:], in_=xw[1][:].indirect(offs_t[:]))
-        round_w1(nc.scalar.copy, 1, 0, 0)
-        round_w1(nc.scalar.copy, 1, 0, 1)
-        round_w1(nc.vector.tensor_copy, 1, 1, 0)
-        round_w1(nc.scalar.copy, 1, 1, 1)
+        gw1 = new([P, S], U32, "gw1", "gw1")
+        gw[1] = [gw1[:, c * BANK : (c + 1) * BANK] for c in range(2)]
+        nc.vector.tensor_copy(out=gw1[:], in_=xw[1][:].indirect(offs_t[:]))
+        for e in range(2):
+            for u in range(2):
+                round_w1(1, e, u)
         quantise_w1(1, 0)
         quantise_w1(1, 1)
         for t in range(PACK):
@@ -132,11 +138,11 @@ def tile_picked_zunm_none_po_kernel(
         h = [new([P, S], F32, "h%d" % t) for t in range(PACK)]
         for t in range(PACK):
             for c in range(2):
-                copy = nc.vector.tensor_copy if (c == 1 and t < 3) else nc.scalar.copy
+                copy = nc.vector.tensor_copy if c == 1 else nc.scalar.copy
                 copy(out=h[t][:, c * BANK : (c + 1) * BANK], in_=h_ps[t][c][:])
 
         w2w = new([P, 2 * N], U8, "w2w")
-        w2s = new([P, N], U8, "w2s")
+        w2s = new([P, N], U8, "w2s", "gw1")
         nc.scalar.copy(
             out=w2w[:].bitcast(U16).rearrange("p (t m) -> p m t", t=PACK),
             in_=w2w_raw[:].bitcast(U16).rearrange("p (m t) -> p m t", t=PACK),
@@ -213,22 +219,24 @@ def tile_picked_zunm_none_po_kernel(
 
         merge(0)
         merge(1)
-        for u in range(2):
-            take_y(0, u)
-            for t in (2 * u, 2 * u + 1):
-                put_first(0, t)
-                put_second(0, t)
-        for u in range(2):
-            take_y(1, u)
-            put_first(1, 2 * u)
-            put_second(1, 2 * u + 1)
-            put_first(1, 2 * u + 1)
-            put_second(1, 2 * u)
-            for t in (2 * u, 2 * u + 1):
-                regroup(nc.sync.dma_start if u == 0 else nc.vector.tensor_copy, t, 0)
-                regroup(nc.sync.dma_start if u == 0 else nc.scalar.copy, t, 1)
-            for t in (2 * u, 2 * u + 1):
-                store(t)
+        take_y(0, 0)
+        take_y(0, 1)
+        for t in range(PACK):
+            put_first(0, t)
+            put_second(0, t)
+        take_y(1, 0)
+        take_y(1, 1)
+        for t in range(PACK):
+            put_first(1, t)
+            put_second(1, t)
+            if t < 2:
+                regroup(nc.sync.dma_start, t, 0)
+                regroup(nc.sync.dma_start, t, 1)
+            store(t)
+        regroup(nc.scalar.copy, 2, 0)
+        regroup(nc.scalar.copy, 2, 1)
+        regroup(nc.vector.tensor_copy, 3, 0)
+        regroup(nc.scalar.copy, 3, 1)
 
         o_codes = new([P, S], U32, "o_codes")
         o_scales = new([P, S], U8, "o_scales")
@@ -244,7 +252,9 @@ def tile_picked_zunm_none_po_kernel(
         for i, (r, c0, w) in enumerate(pieces):
             cols = slice(starts[r] + c0, starts[r] + c0 + w)
             nc.vector.quantize_mx(out=o_codes[:, cols].bitcast(FP8X4), scales=o_scales[:, cols], in_=o_bf[i][:])
-            nc.sync.dma_start(out=words_out[:, cols], in_=o_codes[:, cols].bitcast(I32))
+            if i > 0:
+                done = slice(starts[r], starts[r] + widths[r])
+                nc.sync.dma_start(out=words_out[:, done], in_=o_codes[:, done].bitcast(I32))
         for q in range(4):
             queue = nc.scalar if q % 2 else nc.sync
             queue.dma_start(

@@ -211,8 +211,9 @@ def tile_picked_zunm_none_po_kernel(
                 op=MULT,
             )
 
-        def regroup(move, t, r):
-            move(out=grouped[r][:, t, :], in_=res[t][:, starts[r] : starts[r] + widths[r]])
+        def regroup(move, t, r, c0=0, w=None):
+            w = widths[r] if w is None else w
+            move(out=grouped[r][:, t, c0 : c0 + w], in_=res[t][:, starts[r] + c0 : starts[r] + c0 + w])
 
         def store(t):
             nc.sync.dma_start(out=out_rows[:, t, :], in_=res[t][:])
@@ -235,12 +236,13 @@ def tile_picked_zunm_none_po_kernel(
             store(t)
         regroup(nc.scalar.copy, 2, 0)
         regroup(nc.scalar.copy, 2, 1)
-        regroup(nc.vector.tensor_copy, 3, 0)
+        regroup(nc.vector.tensor_copy, 3, 0, 0, 256)
+        regroup(nc.vector.tensor_copy, 3, 0, 256, SPLIT - 256)
         regroup(nc.scalar.copy, 3, 1)
 
         o_codes = new([P, S], U32, "o_codes")
         o_scales = new([P, S], U8, "o_scales")
-        pieces = ((0, 0, 256), (0, 256, SPLIT - 256), (1, 0, S - SPLIT))
+        pieces = ((0, 0, 256), (0, 256, SPLIT - 256), (1, 0, 256), (1, 256, S - SPLIT - 256))
         o_bf = [new([P, PACK * w], BF16, "o_bf%d" % i) for i, (r, c0, w) in enumerate(pieces)]
         for i, (r, c0, w) in enumerate(pieces):
             copy = nc.vector.tensor_copy if r == 0 else nc.scalar.copy
@@ -253,7 +255,7 @@ def tile_picked_zunm_none_po_kernel(
             cols = slice(starts[r] + c0, starts[r] + c0 + w)
             nc.vector.quantize_mx(out=o_codes[:, cols].bitcast(FP8X4), scales=o_scales[:, cols], in_=o_bf[i][:])
             if i > 0:
-                done = slice(starts[r], starts[r] + widths[r])
+                done = slice(0, SPLIT) if r == 0 else cols
                 nc.sync.dma_start(out=words_out[:, done], in_=o_codes[:, done].bitcast(I32))
         for q in range(4):
             queue = nc.scalar if q % 2 else nc.sync

from contextlib import ExitStack

import concourse.mybir as mybir

K, T, S, H, N, V = 1024, 2048, 1024, 512, 512, 512
FLOPS = 2 * K * H * S + 2 * H * N * V

F32 = mybir.dt.float32
BF16 = mybir.dt.bfloat16
I32 = mybir.dt.int32
U32 = mybir.dt.uint32
U16 = mybir.dt.uint16
U8 = mybir.dt.uint8
FP8X4 = mybir.dt.float8_e4m3fn_x4
FP4X4 = mybir.dt.float4_e2m1fn_x4
MULT = mybir.AluOpType.mult
ADD = mybir.AluOpType.add
COPY = mybir.ActivationFunctionType.Copy

P = 128
PACK = 4
PASSES = K // (P * PACK)
BANK = 512
HALF = V // 2
STRIPE = 16
SPLIT = 640


def tile_picked_zunm_none_po_kernel(
    tc, x_words, x_scales, w1, w2_words, w2_scales, gate, back, offs, ka, kb, out_0, out_1, out_2
):
    nc = tc.nc
    with ExitStack() as ctx:
        sb = ctx.enter_context(tc.tile_pool(name="sb", bufs=1))
        psum = ctx.enter_context(tc.psum_pool(name="psum", bufs=1))

        def new(shape, dtype, name, tag=""):
            return sb.tile(shape, dtype, name=name, tag=tag, align_bytes=64)

        offs_t = sb.tile([P, S // STRIPE], U16, name="offs_t")
        ka_t = sb.tile([P, V // STRIPE], U16, name="ka_t")
        kb_t = sb.tile([P, V // STRIPE], U16, name="kb_t")

        xw = [new([P, T], U32, "xw%d" % g) for g in range(PASSES)]
        xs = new([P, T], U8, "xs", "gw1")
        w1_raw = [[new([P, PACK, H // 2], F32, "w1_raw%d%d" % (g, e)) for e in range(2)] for g in range(PASSES)]
        w2w_raw = new([P, 2 * N], U8, "w2w_raw")
        w2s_raw = new([P, N], U8, "w2s_raw")
        gate_t = new([P, V], F32, "gate_t")
        back_t = new([P, V], F32, "back_t")

        def load_x(g):
            nc.sync.dma_start(out=xw[g][:].bitcast(I32), in_=x_words[g].rearrange("p n t -> p (n t)").bitcast(I32))

        def load_w1(g):
            for e in range(2):
                rows = w1[g * 512 : (g + 1) * 512, e * (H // 2) : (e + 1) * (H // 2)]
                nc.sync.dma_start(out=w1_raw[g][e][:], in_=rows.rearrange("(p j) c -> p j c", j=PACK))

        nc.vector.memset(xs[:, :1408].bitcast(I32), 0)
        nc.gpsimd.memset(xs[:, 1408:].bitcast(I32), 0)
        nc.gpsimd.memset(w2s_raw[:].bitcast(I32), 0)
        load_x(0)
        nc.sync.dma_start(out=offs_t[:], in_=offs)
        for q in range(4):
            nc.sync.dma_start(
                out=xs[32 * q : 32 * q + 4 * PASSES, :].bitcast(I32), in_=x_scales[:, 4 * q : 4 * q + 4, :].bitcast(I32)
            )
        load_w1(0)
        load_x(1)
        load_w1(1)
        nc.sync.dma_start(out=w2w_raw[:].bitcast(I32), in_=w2_words[0].bitcast(I32))
        nc.sync.dma_start(out=kb_t[:], in_=kb)
        nc.sync.dma_start(out=ka_t[:], in_=ka)
        nc.sync.dma_start(out=gate_t[:], in_=gate)
        for q in range(4):
            nc.sync.dma_start(
                out=w2s_raw[32 * q : 32 * q + 4, :].bitcast(I32), in_=w2_scales[0, 4 * q : 4 * q + 4, :].bitcast(I32)
            )
        nc.sync.dma_start(out=back_t[:], in_=back)

        w1_bf = [[new([P, 2 * P * PACK], BF16, "w1_bf%d%d" % (g, u), "w1_bf%d%d" % (g, u)) for u in range(2)] for g in range(PASSES)]
        w1_codes = [[new([P, 2 * P], U32, "w1_codes%d%d" % (g, u)) for u in range(2)] for g in range(PASSES)]
        w1_scales = [[new([P, 2 * P], U8, "w1_scales%d%d" % (g, u)) for u in range(2)] for g in range(PASSES)]

        def round_w1(g, e, u):
            nc.scalar.copy(
                out=w1_bf[g][u][:].rearrange("p (t m j) -> p m j t", t=2, j=PACK)[:, e * (P // 2) : (e + 1) * (P // 2), :, :],
                in_=w1_raw[g][e][:].rearrange("p j (m t) -> p m j t", t=PACK)[:, :, :, 2 * u : 2 * u + 2],
            )

        def quantise_w1(g, u):
            nc.vector.quantize_mx(out=w1_codes[g][u][:].bitcast(FP8X4), scales=w1_scales[g][u][:], in_=w1_bf[g][u][:])

        gs = [None, None]
        gw = [[new([P, BANK], U32, "gw0%d" % c)[:] for c in range(2)], None]
        half_list = [offs_t[:, c * (BANK // STRIPE) : (c + 1) * (BANK // STRIPE)] for c in range(2)]
        h_ps = [[psum.tile([P, BANK], F32, name="h_ps%d%d" % (t, c), tag="bank%d" % (2 * t + c)) for c in range(2)] for t in range(PACK)]

        def product1(g, t, c):
            cols = slice((t % 2) * P, (t % 2 + 1) * P)
            nc.tensor.matmul_mx(
                out=h_ps[t][c][:],
                lhsT=w1_codes[g][t // 2][:, cols].bitcast(FP8X4),
                lhsT_scale=w1_scales[g][t // 2][:, cols],
                rhs=gw[g][c].bitcast(FP8X4),
                rhs_scale=gs[c][4 * g : P, :],
                start=(g == 0),
                stop=(g == PASSES - 1),
            )

        for e in range(2):
            for u in range(2):
                round_w1(0, e, u)
        gs[0] = new([P, BANK], U8, "gs0", "gs0")
        nc.vector.tensor_copy(out=gw[0][0], in_=xw[0][:].indirect(half_list[0]))
        nc.vector.tensor_copy(out=gs[0][:], in_=xs[:].indirect(half_list[0]))
        nc.vector.tensor_copy(out=gw[0][1], in_=xw[0][:].indirect(half_list[1]))
        quantise_w1(0, 0)
        quantise_w1(0, 1)
        gs[1] = new([P, BANK], U8, "gs1", "w1_bf00")
        nc.vector.tensor_copy(out=gs[1][:], in_=xs[:].indirect(half_list[1]))
        for c in range(2):
            for t in range(PACK):
                product1(0, t, c)
        gw1 = new([P, S], U32, "gw1", "gw1")
        gw[1] = [gw1[:, c * BANK : (c + 1) * BANK] for c in range(2)]
        nc.vector.tensor_copy(out=gw1[:], in_=xw[1][:].indirect(offs_t[:]))
        for e in range(2):
            for u in range(2):
                round_w1(1, e, u)
        quantise_w1(1, 0)
        quantise_w1(1, 1)
        for t in range(PACK):
            for c in range(2):
                product1(1, t, c)

        h = [new([P, S], F32, "h%d" % t) for t in range(PACK)]
        for t in range(PACK):
            for c in range(2):
                copy = nc.vector.tensor_copy if c == 1 else nc.scalar.copy
                copy(out=h[t][:, c * BANK : (c + 1) * BANK], in_=h_ps[t][c][:])

        w2w = new([P, 2 * N], U8, "w2w")
        w2s = new([P, N], U8, "w2s", "gw1")
        nc.scalar.copy(
            out=w2w[:].bitcast(U16).rearrange("p (t m) -> p m t", t=PACK),
            in_=w2w_raw[:].bitcast(U16).rearrange("p (m t) -> p m t", t=PACK),
        )

        nc.vector.tensor_copy(
            out=w2s[:].rearrange("p (t m) -> p t m", t=PACK), in_=w2s_raw[:].rearrange("p (m t) -> p t m", t=PACK)
        )
        per = HALF // STRIPE
        y = [[new([P, 2 * HALF], F32, "y%d%d" % (a, u)) for u in range(2)] for a in range(2)]
        y_ps = [[None, None], [None, None]]

        def merge(a):
            first = new([P, PACK, HALF], F32, "first%d" % a)
            second = new([P, PACK, HALF], F32, "second")
            z_bf = new([P, HALF * PACK], BF16, "z_bf%d" % a)
            z_codes = new([P, HALF], U32, "z_codes%d" % a)
            z_scales = new([P, HALF], U8, "z_scales%d" % a)
            for t in range(PACK):
                nc.scalar.activation(out=first[:, t, :], in_=h[t][:].indirect(ka_t[:, a * per : (a + 1) * per]), func=COPY)
                nc.vector.tensor_tensor(
                    out=second[:, t, :],
                    in0=h[t][:].indirect(kb_t[:, a * per : (a + 1) * per]),
                    in1=gate_t[:, a * HALF : (a + 1) * HALF],
                    op=MULT,
                )
            nc.vector.tensor_tensor(
                out=z_bf[:].rearrange("p (c i t) -> p c t i", i=4, t=PACK),
                in0=first[:].rearrange("p t (c i) -> p c t i", i=4),
                in1=second[:].rearrange("p t (c i) -> p c t i", i=4),
                op=ADD,
            )
            nc.vector.quantize_mx(out=z_codes[:].bitcast(FP8X4), scales=z_scales[:], in_=z_bf[:])
            for u in range(2):
                y_ps[a][u] = psum.tile([P, BANK], F32, name="y_ps%d%d" % (a, u), tag="bank%d" % (2 * a + u))
                for e in range(2):
                    t = 2 * u + e
                    nc.tensor.matmul_mx(
                        out=y_ps[a][u][:, e * HALF : (e + 1) * HALF],
                        lhsT=w2w[:, 2 * P * t : 2 * P * (t + 1)].bitcast(FP4X4),
                        lhsT_scale=w2s[:, P * t : P * (t + 1)],
                        rhs=z_codes[:].bitcast(FP8X4),
                        rhs_scale=z_scales[:],
                        start=True,
                        stop=True,
                    )

        def take_y(a, u):
            nc.scalar.copy(out=y[a][u][:], in_=y_ps[a][u][:])

        res = [new([P, S], F32, "res%d" % t) for t in range(PACK)]
        widths = (SPLIT, S - SPLIT)
        starts = (0, SPLIT)
        grouped = [new([P, PACK, widths[r]], F32, "grouped%d" % r) for r in range(2)]
        out_rows = out_0.rearrange("(p t) s -> p t s", t=PACK)

        def put_first(a, t):
            src = y[a][t // 2][:, (t % 2) * HALF : (t % 2 + 1) * HALF]
            nc.scalar.activation(out=res[t][:].indirect(ka_t[:, a * per : (a + 1) * per]), in_=src, func=COPY)

        def put_second(a, t):
            nc.vector.tensor_tensor(
                out=res[t][:].indirect(kb_t[:, a * per : (a + 1) * per]),
                in0=y[a][t // 2][:, (t % 2) * HALF : (t % 2 + 1) * HALF],
                in1=back_t[:, a * HALF : (a + 1) * HALF],
                op=MULT,
            )

        def regroup(move, t, r, c0=0, w=None):
            w = widths[r] if w is None else w
            move(out=grouped[r][:, t, c0 : c0 + w], in_=res[t][:, starts[r] + c0 : starts[r] + c0 + w])

        def store(t):
            nc.sync.dma_start(out=out_rows[:, t, :], in_=res[t][:])

        merge(0)
        merge(1)
        take_y(0, 0)
        take_y(0, 1)
        for t in range(PACK):
            put_first(0, t)
            put_second(0, t)
        take_y(1, 0)
        take_y(1, 1)
        for t in range(PACK):
            put_first(1, t)
            put_second(1, t)
            if t < 2:
                regroup(nc.sync.dma_start, t, 0)
                regroup(nc.sync.dma_start, t, 1)
            store(t)
        regroup(nc.scalar.copy, 2, 0)
        regroup(nc.scalar.copy, 2, 1)
        regroup(nc.vector.tensor_copy, 3, 0, 0, 256)
        regroup(nc.vector.tensor_copy, 3, 0, 256, SPLIT - 256)
        regroup(nc.scalar.copy, 3, 1)

        o_codes = new([P, S], U32, "o_codes")
        o_scales = new([P, S], U8, "o_scales")
        pieces = ((0, 0, 256), (0, 256, SPLIT - 256), (1, 0, 256), (1, 256, S - SPLIT - 256))
        o_bf = [new([P, PACK * w], BF16, "o_bf%d" % i) for i, (r, c0, w) in enumerate(pieces)]
        for i, (r, c0, w) in enumerate(pieces):
            copy = nc.vector.tensor_copy if r == 0 else nc.scalar.copy
            copy(
                out=o_bf[i][:].rearrange("p (c i t) -> p c t i", i=4, t=PACK),
                in_=grouped[r][:, :, c0 : c0 + w].rearrange("p t (c i) -> p c t i", i=4),
            )
        words_out = out_1[0].rearrange("p n t -> p (n t)").bitcast(I32)
        for i, (r, c0, w) in enumerate(pieces):
            cols = slice(starts[r] + c0, starts[r] + c0 + w)
            nc.vector.quantize_mx(out=o_codes[:, cols].bitcast(FP8X4), scales=o_scales[:, cols], in_=o_bf[i][:])
            if i > 0:
                done = slice(0, SPLIT) if r == 0 else cols
                nc.sync.dma_start(out=words_out[:, done], in_=o_codes[:, done].bitcast(I32))
        for q in range(4):
            queue = nc.scalar if q % 2 else nc.sync
            queue.dma_start(
                out=out_2[0, 4 * q : 4 * q + 4, :].bitcast(I32), in_=o_scales[32 * q : 32 * q + 4, :].bitcast(I32)
            )
